import numpy as np, ml_dtypes
CORES = [1,2,5,7,57,58,61,63,73,74,77,79]
N = 12
F = 256
def setup_inputs(rng):
    m = (rng.standard_normal((N, 128, 128), dtype=np.float32) / 11).astype(ml_dtypes.bfloat16)
    return {"m": m, "mt": m.transpose(0, 2, 1).copy(), "x": rng.standard_normal((N, 128, F), dtype=np.float32).astype(ml_dtypes.bfloat16)}
def setup_inputs_big(rng):
    d = setup_inputs(rng)
    for k in ("x",): d[k] = (d[k].astype(np.float32) * 1048576.0).astype(d[k].dtype)
    return d
def setup_inputs_small(rng):
    d = setup_inputs(rng)
    for k in ("x",): d[k] = (d[k].astype(np.float32) * (1 / 1048576.0)).astype(d[k].dtype)
    return d
def setup_inputs_apart(rng):
    d = setup_inputs(rng)
    f = (10.0 ** rng.permutation(np.linspace(-1.5, 1.5, N))).astype(np.float32).reshape(N, 1, 1)
    for k in ("x",): d[k] = (d[k].astype(np.float32) * f).astype(d[k].dtype)
    return d
def reference(m, mt, x):
    M, X = m.astype(np.float64), x.astype(np.float64)
    y = np.zeros((N, 128, F)); p = X[0]
    for r in range(N):
        p = M[r].T @ p
        y[r] = p
    return {"y": y.astype(ml_dtypes.bfloat16)}

@@ -1,0 +1,159 @@
+from concourse.bass import DstId, RemoteDMATransfer
+
+D = 128
+F = 256
+NSTEP = 6
+
+SCRATCH = {
+    "own_m": ("sbuf", [D, D], "bfloat16"),
+    "own_mt": ("sbuf", [D, D], "bfloat16"),
+    "xin": ("sbuf", [D, F], "bfloat16"),
+    "pin": ("sbuf", [D, F], "bfloat16"),
+    "pout": ("sbuf", [D, F], "bfloat16"),
+    "psend": ("sbuf", [D, F], "bfloat16"),
+    "et": ("sbuf", [D, D], "bfloat16"),
+}
+for _k in range(12):
+    SCRATCH["a%d" % _k] = ("sbuf", [D, D], "bfloat16")
+for _k in range(NSTEP):
+    SCRATCH["w%d" % _k] = ("sbuf", [D, D], "bfloat16")
+    SCRATCH["ps%d" % _k] = ("psum", [D, 512], "float32")
+
+SEMAPHORES = (["ld_m", "ld_mt", "ld_x", "st", "sent", "in_p", "in_e"]
+              + ["sa%d" % k for k in range(12)]
+              + ["t%d" % k for k in range(NSTEP)] + ["v%d" % k for k in range(NSTEP)])
+
+FORM = {1: "mt", 2: "mt", 3: "m", 4: "mt", 5: "m", 6: "mt", 7: "m", 8: "mt", 9: "mt", 10: "mt"}
+NEED = {1: [2, 3], 2: [1], 3: [1, 2],
+        4: [5, 6, 7], 5: [4, 6, 7], 6: [4, 5, 7], 7: [4, 5, 6],
+        9: [8], 10: [8, 9], 11: [8, 9, 10]}
+LOADS_MT = (1, 2, 4, 6, 8, 9, 10)
+
+
+def _count(mask):
+    return sum((mask >> e) & 1 for e in range(16))
+
+
+def rank_program(g, core, T, topo):
+    rank = T.rank_of(core)
+    if rank is None:
+        return
+    cores = list(T.cores)
+    far = [r for r in range(len(cores)) if topo.chip(cores[r]) != topo.chip(cores[0])]
+    senders = [r for r in range(1, 4) if all(topo.may_write(cores[r], cores[d]) for d in far)]
+    takes = {s: [d for d in far if topo.die(cores[d]) == topo.die(cores[s])] for s in senders}
+
+    sent = [0]
+
+    def send(src, dst, ranks, sem):
+        mask = topo.mask(core, cores[ranks[0]])
+        ids = []
+        for r in ranks:
+            mask &= topo.mask(core, cores[r])
+            rid, pid, _ = topo.addr(cores[r])
+            ids.append(DstId(rid=rid, pnc=pid))
+        g.remote_dma_fused([RemoteDMATransfer(dst_ids=ids, dma_engine_mask=mask, remote_sem=T.sem[sem],
+                                              srcs=[src], dsts=[dst for _ in ranks], alu_op=0)],
+                           local_sem=T.sem.sent)
+        sent[0] += _count(mask)
+
+    def lands(src_rank):
+        return _count(topo.mask(cores[src_rank], core))
+
+    own = {}
+    if rank in LOADS_MT:
+        g.sync.dma_start(T.own_mt[:], T.mt[:]).then_inc(T.sem.ld_mt, 16)
+        own["mt"] = (T.own_mt[:], [("ld_mt", 16)], D)
+        g.scalar.dma_start(T.own_m[:], T.m[:]).then_inc(T.sem.ld_m, 16)
+    elif rank == 0:
+        g.sync.dma_start(T.xin[:], T.x[:]).then_inc(T.sem.ld_x, 16)
+        g.scalar.dma_start(T.own_m[:], T.m[:]).then_inc(T.sem.ld_m, 16)
+    else:
+        g.sync.dma_start(T.own_m[:], T.m[:]).then_inc(T.sem.ld_m, 16)
+    own["m"] = (T.own_m[:], [("ld_m", 16)], D)
+
+    def after(opnd):
+        for s, v in opnd[1]:
+            g.wait_ge(T.sem[s], v)
+
+    if rank in FORM:
+        after(own[FORM[rank]])
+        send(own[FORM[rank]][0], T["a%d" % rank][:], [r for r in sorted(NEED) if rank in NEED[r]], "sa%d" % rank)
+
+    def mat(k, form):
+        if k == rank:
+            return own[form]
+        return (T["a%d" % k][:], [("sa%d" % k, lands(k))], D)
+
+    step = [0]
+    waited = set()
+
+    def mm(lhsT, rhs, out=None):
+        k = step[0]
+        step[0] += 1
+        n = rhs[2]
+        if out is None:
+            out = T["w%d" % k][:]
+        for s, v in lhsT[1] + rhs[1]:
+            if (s, v) not in waited:
+                waited.add((s, v))
+                g.tensor.wait_ge(T.sem[s], v)
+        acc = T["ps%d" % k][:, 0:n]
+        g.tensor.matmul(acc, lhsT[0], rhs[0], start=True, stop=True).then_inc(T.sem["t%d" % k], 1)
+        g.vector.wait_ge(T.sem["t%d" % k], 1)
+        g.vector.tensor_copy(out, acc).then_inc(T.sem["v%d" % k], 1)
+        return (out, [("v%d" % k, 1)], n)
+
+    def store(y):
+        for s, v in y[1]:
+            g.sync.wait_ge(T.sem[s], v)
+        g.sync.dma_start(T.y[:], y[0]).then_inc(T.sem.st, 16)
+        g.sync.wait_ge(T.sem.st, 16)
+
+    if rank == 0:
+        y = mm(own["m"], (T.xin[:], [("ld_x", 16)], F), T.pout[:])
+        after(y)
+        send(y[0], T.pin[:], senders, "in_p")
+        send(y[0], T.pin[:], [r for r in range(1, 4) if r not in senders], "in_p")
+        store(y)
+    elif rank < 4:
+        p0 = (T.pin[:], [("in_p", lands(0))], F)
+        p3 = None
+        if rank in senders:
+            t = mm(mat(1, "mt"), mm(mat(2, "mt"), mat(3, "m")))
+            p3 = mm(t, p0, T.pout[:] if rank == 3 else T.psend[:])
+            after(p3)
+            send(p3[0], T.pin[:], takes[rank], "in_p")
+        if rank == 1:
+            y = mm(own["m"], p0, T.pout[:])
+        elif rank == 2:
+            y = mm(mm(mat(1, "mt"), own["m"]), p0, T.pout[:])
+        else:
+            y = p3
+        store(y)
+    else:
+        sender = [s for s in senders if rank in takes[s]][0]
+        p3 = (T.pin[:], [("in_p", lands(sender))], F)
+        if rank < 8:
+            at = mm(mat(5, "m"), mat(4, "mt"))
+            b = mm(mat(6, "mt"), mat(7, "m"))
+            et = mm(b, at)
+            after(et)
+            send(et[0], T.et[:], [rank + 4], "in_e")
+            if rank == 4:
+                q = own["m"]
+            elif rank == 5:
+                q = mm(mat(4, "mt"), own["m"])
+            elif rank == 6:
+                q = mm(at, own["m"])
+            else:
+                q = mm(at, b)
+        else:
+            q = own["m"]
+            for k in range(rank - 1, 7, -1):
+                q = mm(mat(k, "mt"), q)
+            q = mm((T.et[:], [("in_e", lands(rank - 4))], D), q)
+        store(mm(q, p3, T.pout[:]))
+
+    if sent[0]:
+        g.wait_ge(T.sem.sent, sent[0])

@@ -3,6 +3,7 @@ from concourse.bass import DstId, RemoteDMATransfer
 D = 128
 F = 256
 NSTEP = 6
+NBANK = 8
 
 SCRATCH = {
     "own_m": ("sbuf", [D, D], "bfloat16"),
@@ -17,11 +18,12 @@ for _k in range(12):
     SCRATCH["a%d" % _k] = ("sbuf", [D, D], "bfloat16")
 for _k in range(NSTEP):
     SCRATCH["w%d" % _k] = ("sbuf", [D, D], "bfloat16")
+for _k in range(NBANK):
     SCRATCH["ps%d" % _k] = ("psum", [D, 512], "float32")
 
 SEMAPHORES = (["ld_m", "ld_mt", "ld_x", "st", "sent", "in_p", "in_e"]
               + ["sa%d" % k for k in range(12)]
-              + ["t%d" % k for k in range(NSTEP)] + ["v%d" % k for k in range(NSTEP)])
+              + ["t%d" % k for k in range(NBANK)] + ["v%d" % k for k in range(NSTEP)])
 
 FORM = {1: "mt", 2: "mt", 3: "m", 4: "mt", 5: "m", 6: "mt", 7: "m", 8: "mt", 9: "mt", 10: "mt"}
 NEED = {1: [2, 3], 2: [1], 3: [1, 2],
@@ -42,10 +44,13 @@ def rank_program(g, core, T, topo):
     far = [r for r in range(len(cores)) if topo.chip(cores[r]) != topo.chip(cores[0])]
     senders = [r for r in range(1, 4) if all(topo.may_write(cores[r], cores[d]) for d in far)]
     takes = {s: [d for d in far if topo.die(cores[d]) == topo.die(cores[s])] for s in senders}
+    passes = {takes[s][0]: takes[s][1] for s in senders}
 
     sent = [0]
 
-    def send(src, dst, ranks, sem):
+    def send(opnd, dst, ranks, sem):
+        for s, v in opnd[1]:
+            g.wait_ge(T.sem[s], v)
         mask = topo.mask(core, cores[ranks[0]])
         ids = []
         for r in ranks:
@@ -53,7 +58,7 @@ def rank_program(g, core, T, topo):
             rid, pid, _ = topo.addr(cores[r])
             ids.append(DstId(rid=rid, pnc=pid))
         g.remote_dma_fused([RemoteDMATransfer(dst_ids=ids, dma_engine_mask=mask, remote_sem=T.sem[sem],
-                                              srcs=[src], dsts=[dst for _ in ranks], alu_op=0)],
+                                              srcs=[opnd[0][:]], dsts=[dst[:] for _ in ranks], alu_op=0)],
                            local_sem=T.sem.sent)
         sent[0] += _count(mask)
 
@@ -63,29 +68,28 @@ def rank_program(g, core, T, topo):
     own = {}
     if rank in LOADS_MT:
         g.sync.dma_start(T.own_mt[:], T.mt[:]).then_inc(T.sem.ld_mt, 16)
-        own["mt"] = (T.own_mt[:], [("ld_mt", 16)], D)
+        own["mt"] = (T.own_mt, [("ld_mt", 16)], D)
+        g.scalar.wait_ge(T.sem.ld_mt, 16)
         g.scalar.dma_start(T.own_m[:], T.m[:]).then_inc(T.sem.ld_m, 16)
     elif rank == 0:
         g.sync.dma_start(T.xin[:], T.x[:]).then_inc(T.sem.ld_x, 16)
         g.scalar.dma_start(T.own_m[:], T.m[:]).then_inc(T.sem.ld_m, 16)
     else:
         g.sync.dma_start(T.own_m[:], T.m[:]).then_inc(T.sem.ld_m, 16)
-    own["m"] = (T.own_m[:], [("ld_m", 16)], D)
-
-    def after(opnd):
-        for s, v in opnd[1]:
-            g.wait_ge(T.sem[s], v)
+    own["m"] = (T.own_m, [("ld_m", 16)], D)
 
     if rank in FORM:
-        after(own[FORM[rank]])
-        send(own[FORM[rank]][0], T["a%d" % rank][:], [r for r in sorted(NEED) if rank in NEED[r]], "sa%d" % rank)
+        to = [r for r in sorted(NEED) if rank in NEED[r]]
+        send(own[FORM[rank]], T["a%d" % rank],
+             [r for r in to if r in senders] + [r for r in to if r not in senders], "sa%d" % rank)
 
     def mat(k, form):
         if k == rank:
             return own[form]
-        return (T["a%d" % k][:], [("sa%d" % k, lands(k))], D)
+        return (T["a%d" % k], [("sa%d" % k, lands(k))], D)
 
     step = [0]
+    bank = [0]
     waited = set()
 
     def mm(lhsT, rhs, out=None):
@@ -93,53 +97,62 @@ def rank_program(g, core, T, topo):
         step[0] += 1
         n = rhs[2]
         if out is None:
-            out = T["w%d" % k][:]
+            out = T["w%d" % k]
         for s, v in lhsT[1] + rhs[1]:
             if (s, v) not in waited:
                 waited.add((s, v))
                 g.tensor.wait_ge(T.sem[s], v)
-        acc = T["ps%d" % k][:, 0:n]
-        g.tensor.matmul(acc, lhsT[0], rhs[0], start=True, stop=True).then_inc(T.sem["t%d" % k], 1)
-        g.vector.wait_ge(T.sem["t%d" % k], 1)
-        g.vector.tensor_copy(out, acc).then_inc(T.sem["v%d" % k], 1)
-        return (out, [("v%d" % k, 1)], n)
+        parts = 2 if n == F else 1
+        w = n // parts
+        used = []
+        for h in range(parts):
+            b = bank[0]
+            bank[0] += 1
+            used.append(b)
+            g.tensor.matmul(T["ps%d" % b][:, 0:w], lhsT[0][:], rhs[0][:, h * w:(h + 1) * w],
+                            start=True, stop=True).then_inc(T.sem["t%d" % b], 1)
+        for h in range(parts):
+            b = used[h]
+            g.vector.wait_ge(T.sem["t%d" % b], 1)
+            g.vector.tensor_copy(out[:, h * w:(h + 1) * w], T["ps%d" % b][:, 0:w]).then_inc(T.sem["v%d" % k], 1)
+        return (out, [("v%d" % k, parts)], n)
 
     def store(y):
         for s, v in y[1]:
             g.sync.wait_ge(T.sem[s], v)
-        g.sync.dma_start(T.y[:], y[0]).then_inc(T.sem.st, 16)
+        g.sync.dma_start(T.y[:], y[0][:]).then_inc(T.sem.st, 16)
         g.sync.wait_ge(T.sem.st, 16)
 
     if rank == 0:
-        y = mm(own["m"], (T.xin[:], [("ld_x", 16)], F), T.pout[:])
-        after(y)
-        send(y[0], T.pin[:], senders, "in_p")
-        send(y[0], T.pin[:], [r for r in range(1, 4) if r not in senders], "in_p")
+        y = mm(own["m"], (T.xin, [("ld_x", 16)], F), T.pout)
+        send(y, T.pin, senders, "in_p")
+        send(y, T.pin, [r for r in range(1, 4) if r not in senders], "in_p")
         store(y)
     elif rank < 4:
-        p0 = (T.pin[:], [("in_p", lands(0))], F)
+        p0 = (T.pin, [("in_p", lands(0))], F)
         p3 = None
         if rank in senders:
             t = mm(mat(1, "mt"), mm(mat(2, "mt"), mat(3, "m")))
-            p3 = mm(t, p0, T.pout[:] if rank == 3 else T.psend[:])
-            after(p3)
-            send(p3[0], T.pin[:], takes[rank], "in_p")
+            p3 = mm(t, p0, T.pout if rank == 3 else T.psend)
+            send(p3, T.pin, [d for d in takes[rank] if d not in passes.values()], "in_p")
         if rank == 1:
-            y = mm(own["m"], p0, T.pout[:])
+            y = mm(own["m"], p0, T.pout)
         elif rank == 2:
-            y = mm(mm(mat(1, "mt"), own["m"]), p0, T.pout[:])
+            y = mm(mm(mat(1, "mt"), own["m"]), p0, T.pout)
         else:
             y = p3
         store(y)
     else:
-        sender = [s for s in senders if rank in takes[s]][0]
-        p3 = (T.pin[:], [("in_p", lands(sender))], F)
+        source = [s for s in senders if rank in takes[s]][0]
+        for a in passes:
+            if passes[a] == rank:
+                source = a
+        p3 = (T.pin, [("in_p", lands(source))], F)
         if rank < 8:
             at = mm(mat(5, "m"), mat(4, "mt"))
             b = mm(mat(6, "mt"), mat(7, "m"))
             et = mm(b, at)
-            after(et)
-            send(et[0], T.et[:], [rank + 4], "in_e")
+            send(et, T.et, [rank + 4], "in_e")
             if rank == 4:
                 q = own["m"]
             elif rank == 5:
@@ -152,8 +165,10 @@ def rank_program(g, core, T, topo):
             q = own["m"]
             for k in range(rank - 1, 7, -1):
                 q = mm(mat(k, "mt"), q)
-            q = mm((T.et[:], [("in_e", lands(rank - 4))], D), q)
-        store(mm(q, p3, T.pout[:]))
+            q = mm((T.et, [("in_e", lands(rank - 4))], D), q)
+        if rank in passes:
+            send(p3, T.pin, [passes[rank]], "in_p")
+        store(mm(q, p3, T.pout))
 
     if sent[0]:
         g.wait_ge(T.sem.sent, sent[0])

from concourse.bass import DstId, RemoteDMATransfer

D = 128
F = 256
NSTEP = 6
NBANK = 8

SCRATCH = {
    "own_m": ("sbuf", [D, D], "bfloat16"),
    "own_mt": ("sbuf", [D, D], "bfloat16"),
    "xin": ("sbuf", [D, F], "bfloat16"),
    "pin": ("sbuf", [D, F], "bfloat16"),
    "pout": ("sbuf", [D, F], "bfloat16"),
    "psend": ("sbuf", [D, F], "bfloat16"),
    "et": ("sbuf", [D, D], "bfloat16"),
}
for _k in range(12):
    SCRATCH["a%d" % _k] = ("sbuf", [D, D], "bfloat16")
for _k in range(NSTEP):
    SCRATCH["w%d" % _k] = ("sbuf", [D, D], "bfloat16")
for _k in range(NBANK):
    SCRATCH["ps%d" % _k] = ("psum", [D, 512], "float32")

SEMAPHORES = (["ld_m", "ld_mt", "ld_x", "st", "sent", "in_p", "in_e"]
              + ["sa%d" % k for k in range(12)]
              + ["t%d" % k for k in range(NBANK)] + ["v%d" % k for k in range(NSTEP)])

FORM = {1: "mt", 2: "mt", 3: "m", 4: "mt", 5: "m", 6: "mt", 7: "m", 8: "mt", 9: "mt", 10: "mt"}
NEED = {1: [2, 3], 2: [1], 3: [1, 2],
        4: [5, 6, 7], 5: [4, 6, 7], 6: [4, 5, 7], 7: [4, 5, 6],
        9: [8], 10: [8, 9], 11: [8, 9, 10]}
LOADS_MT = (1, 2, 4, 6, 8, 9, 10)


def _count(mask):
    return sum((mask >> e) & 1 for e in range(16))


def rank_program(g, core, T, topo):
    rank = T.rank_of(core)
    if rank is None:
        return
    cores = list(T.cores)
    far = [r for r in range(len(cores)) if topo.chip(cores[r]) != topo.chip(cores[0])]
    senders = [r for r in range(1, 4) if all(topo.may_write(cores[r], cores[d]) for d in far)]
    takes = {s: [d for d in far if topo.die(cores[d]) == topo.die(cores[s])] for s in senders}
    passes = {takes[s][0]: takes[s][1] for s in senders}

    sent = [0]

    def send(opnd, dst, ranks, sem):
        for s, v in opnd[1]:
            g.wait_ge(T.sem[s], v)
        mask = topo.mask(core, cores[ranks[0]])
        ids = []
        for r in ranks:
            mask &= topo.mask(core, cores[r])
            rid, pid, _ = topo.addr(cores[r])
            ids.append(DstId(rid=rid, pnc=pid))
        g.remote_dma_fused([RemoteDMATransfer(dst_ids=ids, dma_engine_mask=mask, remote_sem=T.sem[sem],
                                              srcs=[opnd[0][:]], dsts=[dst[:] for _ in ranks], alu_op=0)],
                           local_sem=T.sem.sent)
        sent[0] += _count(mask)

    def lands(src_rank):
        return _count(topo.mask(cores[src_rank], core))

    own = {}
    if rank in LOADS_MT:
        g.sync.dma_start(T.own_mt[:], T.mt[:]).then_inc(T.sem.ld_mt, 16)
        own["mt"] = (T.own_mt, [("ld_mt", 16)], D)
        g.scalar.wait_ge(T.sem.ld_mt, 16)
        g.scalar.dma_start(T.own_m[:], T.m[:]).then_inc(T.sem.ld_m, 16)
    elif rank == 0:
        g.sync.dma_start(T.xin[:], T.x[:]).then_inc(T.sem.ld_x, 16)
        g.scalar.dma_start(T.own_m[:], T.m[:]).then_inc(T.sem.ld_m, 16)
    else:
        g.sync.dma_start(T.own_m[:], T.m[:]).then_inc(T.sem.ld_m, 16)
    own["m"] = (T.own_m, [("ld_m", 16)], D)

    if rank in FORM:
        to = [r for r in sorted(NEED) if rank in NEED[r]]
        send(own[FORM[rank]], T["a%d" % rank],
             [r for r in to if r in senders] + [r for r in to if r not in senders], "sa%d" % rank)

    def mat(k, form):
        if k == rank:
            return own[form]
        return (T["a%d" % k], [("sa%d" % k, lands(k))], D)

    step = [0]
    bank = [0]
    waited = set()

    def mm(lhsT, rhs, out=None):
        k = step[0]
        step[0] += 1
        n = rhs[2]
        if out is None:
            out = T["w%d" % k]
        for s, v in lhsT[1] + rhs[1]:
            if (s, v) not in waited:
                waited.add((s, v))
                g.tensor.wait_ge(T.sem[s], v)
        parts = 2 if n == F else 1
        w = n // parts
        used = []
        for h in range(parts):
            b = bank[0]
            bank[0] += 1
            used.append(b)
            g.tensor.matmul(T["ps%d" % b][:, 0:w], lhsT[0][:], rhs[0][:, h * w:(h + 1) * w],
                            start=True, stop=True).then_inc(T.sem["t%d" % b], 1)
        for h in range(parts):
            b = used[h]
            g.vector.wait_ge(T.sem["t%d" % b], 1)
            g.vector.tensor_copy(out[:, h * w:(h + 1) * w], T["ps%d" % b][:, 0:w]).then_inc(T.sem["v%d" % k], 1)
        return (out, [("v%d" % k, parts)], n)

    def store(y):
        for s, v in y[1]:
            g.sync.wait_ge(T.sem[s], v)
        g.sync.dma_start(T.y[:], y[0][:]).then_inc(T.sem.st, 16)
        g.sync.wait_ge(T.sem.st, 16)

    if rank == 0:
        y = mm(own["m"], (T.xin, [("ld_x", 16)], F), T.pout)
        send(y, T.pin, senders, "in_p")
        send(y, T.pin, [r for r in range(1, 4) if r not in senders], "in_p")
        store(y)
    elif rank < 4:
        p0 = (T.pin, [("in_p", lands(0))], F)
        p3 = None
        if rank in senders:
            t = mm(mat(1, "mt"), mm(mat(2, "mt"), mat(3, "m")))
            p3 = mm(t, p0, T.pout if rank == 3 else T.psend)
            send(p3, T.pin, [d for d in takes[rank] if d not in passes.values()], "in_p")
        if rank == 1:
            y = mm(own["m"], p0, T.pout)
        elif rank == 2:
            y = mm(mm(mat(1, "mt"), own["m"]), p0, T.pout)
        else:
            y = p3
        store(y)
    else:
        source = [s for s in senders if rank in takes[s]][0]
        for a in passes:
            if passes[a] == rank:
                source = a
        p3 = (T.pin, [("in_p", lands(source))], F)
        if rank < 8:
            at = mm(mat(5, "m"), mat(4, "mt"))
            b = mm(mat(6, "mt"), mat(7, "m"))
            et = mm(b, at)
            send(et, T.et, [rank + 4], "in_e")
            if rank == 4:
                q = own["m"]
            elif rank == 5:
                q = mm(mat(4, "mt"), own["m"])
            elif rank == 6:
                q = mm(at, own["m"])
            else:
                q = mm(at, b)
        else:
            q = own["m"]
            for k in range(rank - 1, 7, -1):
                q = mm(mat(k, "mt"), q)
            q = mm((T.et, [("in_e", lands(rank - 4))], D), q)
        if rank in passes:
            send(p3, T.pin, [passes[rank]], "in_p")
        store(mm(q, p3, T.pout))

    if sent[0]:
        g.wait_ge(T.sem.sent, sent[0])
